import numpy as np
import ml_dtypes


def mxq(x, axis, fmt="e4m3"):
    dtype, down = {"e4m3": (ml_dtypes.float8_e4m3fn, 7), "e5m2": (ml_dtypes.float8_e5m2, 14)}[fmt]
    v = np.moveaxis(np.asarray(x, np.float32).astype(ml_dtypes.bfloat16).astype(np.float64), axis, -1)
    blocks = v.reshape(v.shape[:-1] + (-1, 32))
    amax = np.abs(blocks).max(-1, keepdims=True)
    byte = np.maximum(np.where(amax > 0, np.frexp(amax)[1] - 1 + 127, 0) - down, 1)
    scale = np.exp2(byte - 127.0)
    codes = (blocks / scale).astype(np.float32).astype(dtype).astype(np.float64)
    return np.moveaxis((codes * scale).reshape(v.shape), -1, axis)


WIDE = False


def mx_kscale(k):
    if not WIDE:
        return np.ones(k)
    levels = np.array([10, -10, 5, -5, 0])
    if k % 512:
        return np.exp2(np.random.permutation(np.resize(levels, k // 32))).repeat(32)
    a = np.empty((k // 512, 16))
    for p in range(k // 512):
        a[p, :8] = np.random.permutation(np.resize(levels, 8))
        for g in range(8):
            far = levels[np.abs(levels - a[p, g]) >= 10]
            a[p, g + 8] = far[np.random.randint(len(far))]
    return np.exp2(a.ravel()).repeat(32)


def f64(x):
    return np.asarray(x).astype(np.float64)


def striped(idx):
    return np.tile(idx.reshape(-1, 16).T, (8, 1)).astype(np.uint16)


def unstriped(offs):
    return offs[:16].T.reshape(-1).astype(np.int64)


def pack_weight(w):
    k, n = w.shape
    w = f64(np.asarray(w, np.float32).astype(ml_dtypes.bfloat16)).reshape(k // 32, 32, n)
    amax = np.abs(w).max(1)
    byte = np.clip(np.where(amax > 0, np.frexp(amax)[1] - 1 + 127 - 7, 1), 1, 254)
    scaled = (w * np.exp2(127.0 - byte)[:, None, :]).reshape(k, n).astype(np.float32)
    words = np.ascontiguousarray(scaled.reshape(k // 512, 128, 4, n).transpose(0, 1, 3, 2)).astype(ml_dtypes.float8_e4m3fn).view(np.uint8)
    return words, np.ascontiguousarray(byte.astype(np.uint8).reshape(k // 512, 16, n))


def unpack_weight(words, scales):
    g, p, n, _ = words.shape
    vals = np.ascontiguousarray(words).view(ml_dtypes.float8_e4m3fn).astype(np.float64) * np.repeat(np.exp2(scales.astype(np.float64) - 127.0), 8, axis=1)[..., None]
    return vals.transpose(0, 1, 3, 2).reshape(g * 512, n)


K, T, S, N = 1024, 2048, 512, 256
P = 2 ** 7


def setup_inputs():
    n = np.random.standard_normal
    s = mx_kscale(K)[:, None]
    packed_xT = pack_weight(n((K, T)) * s)
    return {
        "x_words": packed_xT[0],
        "x_scales": packed_xT[1],
        "wc0": (n((K, N)) / np.sqrt(K) / s).astype(np.float32),
        "wd0": (n((K, N)) / np.sqrt(K) / s).astype(np.float32),
        "ideal0": (np.tile(np.random.uniform(0.1, 0.6, S), (P, 1))).astype(np.float32),
        "wc1": (n((K, N)) / np.sqrt(K) / s).astype(np.float32),
        "wd1": (n((K, N)) / np.sqrt(K) / s).astype(np.float32),
        "ideal1": (np.tile(np.random.uniform(0.1, 0.6, S), (P, 1))).astype(np.float32),
        "wc2": (n((K, N)) / np.sqrt(K) / s).astype(np.float32),
        "wd2": (n((K, N)) / np.sqrt(K) / s).astype(np.float32),
        "ideal2": (np.tile(np.random.uniform(0.1, 0.6, S), (P, 1))).astype(np.float32),
        "ref": (n((N, S))).astype(np.float32),
        "offs": striped(np.random.permutation(T)[:S]),
    }


def reference(x_words, x_scales, wc0, wd0, ideal0, wc1, wd1, ideal1, wc2, wd2, ideal2, ref, offs):
    xq = unpack_weight(x_words, x_scales)[:, unstriped(offs)]
    rec0 = mxq(f64(wc0), 0, "e4m3").T @ xq
    a0 = f64(ideal0)[:1] / ((((mxq(f64(wd0), 0, "e4m3").T @ xq)) ** 2 + 0.3) ** 2)
    rec1 = mxq(f64(wc1), 0, "e4m3").T @ xq
    a1 = f64(ideal1)[:1] / ((((mxq(f64(wd1), 0, "e4m3").T @ xq)) ** 2 + 0.3) ** 2)
    rec2 = mxq(f64(wc2), 0, "e4m3").T @ xq
    a2 = f64(ideal2)[:1] / ((((mxq(f64(wd2), 0, "e4m3").T @ xq)) ** 2 + 0.3) ** 2)
    num = rec0 * a0 + rec1 * a1 + rec2 * a2
    den = a0 + a1 + a2
    return np.abs(num / den - f64(ref))

@@ -1,0 +1,268 @@
+from contextlib import ExitStack
+
+import concourse.mybir as mybir
+from concourse.masks import make_identity
+
+K, T, S, N = 1024, 2048, 512, 256
+FLOPS = 6 * 2 * K * N * S
+
+F32 = mybir.dt.float32
+BF16 = mybir.dt.bfloat16
+I32 = mybir.dt.int32
+U32 = mybir.dt.uint32
+U16 = mybir.dt.uint16
+U8 = mybir.dt.uint8
+FP8X4 = mybir.dt.float8_e4m3fn_x4
+ACT = mybir.ActivationFunctionType
+ALU = mybir.AluOpType
+
+P = 128
+PACK = 4
+K_PASS = P * PACK
+PASSES = K // K_PASS
+HALVES = 2
+HALF = S // HALVES
+TILES = HALF // P
+M_TILES = N // P
+EPS = 0.3
+RUN = 4
+
+ON_SCALAR = {("d0", 0), ("d0", 1), ("d1", 0), ("c2", 1), ("c1", 0), ("c1", 1)}
+
+
+def tile_picked_yweno_err_p_kernel(
+    tc, x_words, x_scales, wc0, wd0, ideal0, wc1, wd1, ideal1, wc2, wd2, ideal2, ref, offs, out
+):
+    nc = tc.nc
+    weights = {"d0": wd0, "d1": wd1, "d2": wd2, "c0": wc0, "c1": wc1, "c2": wc2}
+    ideals = (ideal0, ideal1, ideal2)
+
+    with ExitStack() as ctx:
+        keep = ctx.enter_context(tc.tile_pool(name="keep", bufs=1))
+        prod = ctx.enter_context(tc.psum_pool(name="prod", bufs=4))
+        sums = ctx.enter_context(tc.psum_pool(name="sums", bufs=1))
+
+        offsets = keep.tile([P, S // 16], U16, name="offsets")
+        nc.sync.dma_start(offsets[:], offs)
+
+        warm = keep.tile([P, 2], F32, name="warm")
+        nc.vector.memset(warm[:, 0:1], 1.0)
+        nc.scalar.activation(warm[:, 1:2], warm[:, 0:1], ACT.Abs_reciprocal_sqrt)
+
+        scale_table = keep.tile([P, T], U8, name="scale_table", align_bytes=64)
+        nc.gpsimd.memset(scale_table[:].bitcast(I32), 0)
+        ident = keep.tile([P, P], F32, name="ident")
+        make_identity(nc, ident[:])
+        ideal_rows = keep.tile([P, P], F32, name="ideal_rows")
+        nc.gpsimd.memset(ideal_rows[:], 0.0)
+
+        raw = {}
+
+        def load_weight(name, g, pieces=1):
+            tile = keep.tile([P, PACK, N], F32, name=f"raw_{name}_{g}")
+            rows = weights[name][g * K_PASS : (g + 1) * K_PASS, :].rearrange("(p t) m -> p t m", t=PACK)
+            step = PACK // pieces
+            for t0 in range(0, PACK, step):
+                nc.sync.dma_start(tile[:, t0 : t0 + step, :], rows[:, t0 : t0 + step, :])
+            raw[name, g] = tile
+
+        word_table = {}
+
+        def load_words(g, pieces=1):
+            tile = keep.tile([P, T], I32, name=f"word_table_{g}", align_bytes=64)
+            words = x_words[g].rearrange("p c t -> p (c t)").bitcast(I32)
+            step = T // pieces
+            for c0 in range(0, T, step):
+                nc.sync.dma_start(tile[:, c0 : c0 + step], words[:, c0 : c0 + step])
+            word_table[g] = tile
+
+        load_weight("d0", 0, 2)
+        load_words(0, 4)
+        load_weight("d0", 1)
+        for q in range(4):
+            nc.sync.dma_start(
+                scale_table[32 * q : 32 * q + 4 * PASSES, :].bitcast(I32),
+                x_scales[:, 4 * q : 4 * q + 4, :].bitcast(I32),
+            )
+        load_words(1)
+        for name in ("d1", "d2"):
+            for g in range(PASSES):
+                load_weight(name, g)
+        for i in range(3):
+            nc.sync.dma_start(
+                ideal_rows[4 * i : 4 * i + 4, :], ideals[i][0, :].rearrange("(t p) -> t p", p=P)
+            )
+        for name in ("c0", "c2", "c1"):
+            for g in range(PASSES):
+                load_weight(name, g)
+        ref_sb = []
+        for b in range(HALVES):
+            tile = keep.tile([P, M_TILES, HALF], F32, name=f"ref_{b}")
+            nc.sync.dma_start(
+                tile[:], ref[:, b * HALF : (b + 1) * HALF].rearrange("(h p) j -> p h j", p=P)
+            )
+            ref_sb.append(tile)
+
+        w_codes, w_scales = {}, {}
+        grouped = {}
+
+        def cast(name, g):
+            tile = keep.tile([P, N, PACK], BF16, name=f"bf_{name}_{g}", align_bytes=64)
+            dst = tile[:].rearrange("p (c i) t -> p c t i", i=RUN)
+            src = raw[name, g][:].rearrange("p t (c i) -> p c t i", i=RUN)
+            if (name, g) in ON_SCALAR:
+                nc.scalar.copy(dst, src)
+            else:
+                nc.vector.tensor_copy(dst, src)
+            grouped[name, g] = tile
+
+        def quantize(name, g):
+            codes = keep.tile([P, N], U32, name=f"wq_{name}_{g}", align_bytes=64)
+            scales = keep.tile([P, N], U8, name=f"ws_{name}_{g}", align_bytes=64)
+            nc.vector.quantize_mx(
+                out=codes[:].bitcast(FP8X4),
+                scales=scales[:],
+                in_=grouped[name, g][:].rearrange("p m t -> p (m t)"),
+            )
+            w_codes[name, g], w_scales[name, g] = codes, scales
+
+        x_codes = {}
+
+        def gather_words(g, b):
+            tile = keep.tile([P, HALF], U32, name=f"xq_{g}_{b}", align_bytes=64)
+            cols = offsets[:, b * (HALF // 16) : (b + 1) * (HALF // 16)]
+            nc.vector.tensor_copy(tile[:], word_table[g][:].bitcast(U32).indirect(cols))
+            x_codes[g, b] = tile
+
+        x_scale = keep.tile([P, S], U8, name="x_scale", align_bytes=64)
+
+        def product(name, b):
+            bank = prod.tile([P, TILES, N], F32, name="bank")
+            for u in range(TILES):
+                j0 = b * HALF + u * P
+                for g in range(PASSES):
+                    nc.tensor.matmul_mx(
+                        out=bank[:, u, :],
+                        lhsT=x_codes[g, b][:, u * P : (u + 1) * P].bitcast(FP8X4),
+                        lhsT_scale=x_scale[4 * g :, j0 : j0 + P],
+                        rhs=w_codes[name, g][:].bitcast(FP8X4),
+                        rhs_scale=w_scales[name, g][:],
+                        start=(g == 0),
+                        stop=(g == PASSES - 1),
+                    )
+            return bank
+
+        def work(name, b):
+            return keep.tile([P, TILES, N], F32, name=f"{name}_{b}")
+
+        def add_transposed(total, source, first, last):
+            for u in range(TILES):
+                for h in range(M_TILES):
+                    nc.tensor.matmul(
+                        total[:, h, u * P : (u + 1) * P],
+                        source(u, h),
+                        ident[:],
+                        is_transpose=True,
+                        start=(first and u == 0 and h == 0),
+                        stop=(last and u == TILES - 1 and h == M_TILES - 1),
+                    )
+
+        def blocks(tile):
+            return lambda u, h: tile[:, u, h * P : (h + 1) * P]
+
+        cast("d0", 0)
+        quantize("d0", 0)
+        for b in range(HALVES):
+            gather_words(0, b)
+        nc.vector.tensor_copy(x_scale[:], scale_table[:].indirect(offsets[:]))
+        cast("d0", 1)
+        quantize("d0", 1)
+        for b in range(HALVES):
+            gather_words(1, b)
+
+        ideal_bank = sums.tile([P, TILES, N], F32, name="num_1")
+        nc.tensor.transpose(ideal_bank[:, 0, 0:P], ideal_rows[:], ident[:])
+        ideal_cols = keep.tile([P, 12], F32, name="ideal_cols")
+        nc.scalar.copy(ideal_cols[:], ideal_bank[:, 0, 0:12])
+
+        def ideal_col(i, b, u):
+            c = 4 * i + b * TILES + u
+            return ideal_cols[:, c : c + 1]
+
+        def inverse_smoothness(name, b):
+            bank = product(name, b)
+            sq = work("sq_" + name, b)
+            nc.scalar.activation(sq[:], bank[:], ACT.Square)
+            sq2 = work("sq2_" + name, b)
+            nc.scalar.activation(sq2[:], sq[:], ACT.Square, bias=EPS)
+            inv = work("inv_" + name, b)
+            nc.scalar.activation(inv[:], sq2[:], ACT.Abs_reciprocal_sqrt)
+            return inv
+
+        def relative_weight(i, b, pivot_sq, inv):
+            ratio = work(f"ratio_{i}", b)
+            nc.vector.scalar_tensor_tensor(ratio[:], pivot_sq[:], EPS, inv[:], ALU.add, ALU.mult)
+            weight = work(f"weight_{i}", b)
+            for u in range(TILES):
+                nc.vector.scalar_tensor_tensor(
+                    weight[:, u, :], ratio[:, u, :], ideal_col(i, b, u), ratio[:, u, :], ALU.mult, ALU.mult
+                )
+            return weight
+
+        den = [sums.tile([P, M_TILES, HALF], F32, name=f"den_{b}") for b in range(HALVES)]
+        num = [sums.tile([P, M_TILES, HALF], F32, name=f"num_{b}") for b in range(HALVES)]
+
+        def prepare(name):
+            for g in range(PASSES):
+                cast(name, g)
+            for g in range(PASSES):
+                quantize(name, g)
+
+        def weighted_term(name, b, weight, first):
+            bank = product(name, b)
+            term = work("term_" + name, b)
+            nc.vector.tensor_tensor(term[:], bank[:], weight[:], ALU.mult)
+            add_transposed(num[b], blocks(term), first, False)
+
+        prepare("d1")
+        prepare("d2")
+        pivot_sq, weight0, weight2 = [], [], []
+        for b in range(HALVES):
+            inv0 = inverse_smoothness("d0", b)
+            bank = product("d1", b)
+            sq = work("sq_d1", b)
+            nc.scalar.activation(sq[:], bank[:], ACT.Square)
+            pivot_sq.append(sq)
+            weight0.append(relative_weight(0, b, sq, inv0))
+            add_transposed(den[b], lambda u, h: ideal_col(1, b, u).to_broadcast([P, P]), True, False)
+            add_transposed(den[b], blocks(weight0[b]), False, False)
+        for b in range(HALVES):
+            inv2 = inverse_smoothness("d2", b)
+            weight2.append(relative_weight(2, b, pivot_sq[b], inv2))
+            add_transposed(den[b], blocks(weight2[b]), False, True)
+        prepare("c0")
+        prepare("c2")
+        prepare("c1")
+        for b in range(HALVES):
+            root = work("root", b)
+            nc.scalar.activation(root[:], den[b][:], ACT.Abs_reciprocal_sqrt)
+            inv_den = work("inv_den", b)
+            nc.scalar.activation(inv_den[:], root[:], ACT.Square)
+            weighted_term("c0", b, weight0[b], True)
+            weighted_term("c2", b, weight2[b], False)
+            bank = product("c1", b)
+            term = work("term_1", b)
+            for u in range(TILES):
+                nc.scalar.activation(term[:, u, :], bank[:, u, :], ACT.Copy, scale=ideal_col(1, b, u))
+            add_transposed(num[b], blocks(term), False, True)
+            ref_den = work("ref_den", b)
+            nc.vector.tensor_tensor(ref_den[:], den[b][:], ref_sb[b][:], ALU.mult)
+            diff = work("diff", b)
+            nc.vector.tensor_tensor(diff[:], num[b][:], ref_den[:], ALU.subtract)
+            err = work("err", b)
+            nc.vector.tensor_tensor(err[:], diff[:], inv_den[:], ALU.mult)
+            res = work("res", b)
+            nc.scalar.activation(res[:], err[:], ACT.Abs)
+            nc.sync.dma_start(
+                out[:, b * HALF : (b + 1) * HALF].rearrange("(h p) j -> p h j", p=P), res[:]
+            )

@@ -26,8 +26,9 @@ TILES = HALF // P
 M_TILES = N // P
 EPS = 0.3
 RUN = 4
+ORDER = ("d0", "d1", "d2", "c0", "c1", "c2")
 
-ON_SCALAR = {("d0", 0), ("d0", 1), ("d1", 0), ("c2", 1), ("c1", 0), ("c1", 1)}
+ON_SCALAR = {("d0", 0), ("d0", 1), ("c2", 0), ("c2", 1), ("c1", 0), ("c1", 1)}
 
 
 def tile_picked_yweno_err_p_kernel(
@@ -39,7 +40,7 @@ def tile_picked_yweno_err_p_kernel(
 
     with ExitStack() as ctx:
         keep = ctx.enter_context(tc.tile_pool(name="keep", bufs=1))
-        prod = ctx.enter_context(tc.psum_pool(name="prod", bufs=4))
+        prod = ctx.enter_context(tc.psum_pool(name="prod", bufs=1))
         sums = ctx.enter_context(tc.psum_pool(name="sums", bufs=1))
 
         offsets = keep.tile([P, S // 16], U16, name="offsets")
@@ -51,20 +52,17 @@ def tile_picked_yweno_err_p_kernel(
 
         scale_table = keep.tile([P, T], U8, name="scale_table", align_bytes=64)
         nc.gpsimd.memset(scale_table[:].bitcast(I32), 0)
-        ident = keep.tile([P, P], F32, name="ident")
-        make_identity(nc, ident[:])
         ideal_rows = keep.tile([P, P], F32, name="ideal_rows")
         nc.gpsimd.memset(ideal_rows[:], 0.0)
+        ident = keep.tile([P, P], F32, name="ident")
 
         raw = {}
 
-        def load_weight(name, g, pieces=1):
-            tile = keep.tile([P, PACK, N], F32, name=f"raw_{name}_{g}")
+        def load_weight(name, g, t0=0, t1=PACK):
+            if (name, g) not in raw:
+                raw[name, g] = keep.tile([P, PACK, N], F32, name=f"raw_{name}_{g}")
             rows = weights[name][g * K_PASS : (g + 1) * K_PASS, :].rearrange("(p t) m -> p t m", t=PACK)
-            step = PACK // pieces
-            for t0 in range(0, PACK, step):
-                nc.sync.dma_start(tile[:, t0 : t0 + step, :], rows[:, t0 : t0 + step, :])
-            raw[name, g] = tile
+            nc.sync.dma_start(raw[name, g][:, t0:t1, :], rows[:, t0:t1, :])
 
         word_table = {}
 
@@ -76,79 +74,77 @@ def tile_picked_yweno_err_p_kernel(
                 nc.sync.dma_start(tile[:, c0 : c0 + step], words[:, c0 : c0 + step])
             word_table[g] = tile
 
-        load_weight("d0", 0, 2)
-        load_words(0, 4)
-        load_weight("d0", 1)
+        for i in range(3):
+            nc.gpsimd.dma_start(
+                ideal_rows[4 * i : 4 * i + 4, :], ideals[i][0, :].rearrange("(t p) -> t p", p=P)
+            )
+        make_identity(nc, ident[:])
+        load_weight("d0", 0)
+        load_words(0, 2)
         for q in range(4):
             nc.sync.dma_start(
                 scale_table[32 * q : 32 * q + 4 * PASSES, :].bitcast(I32),
                 x_scales[:, 4 * q : 4 * q + 4, :].bitcast(I32),
             )
-        load_words(1)
-        for name in ("d1", "d2"):
+        load_weight("d0", 1)
+        load_words(1, 2)
+        for name in ORDER[1:]:
             for g in range(PASSES):
                 load_weight(name, g)
-        for i in range(3):
-            nc.sync.dma_start(
-                ideal_rows[4 * i : 4 * i + 4, :], ideals[i][0, :].rearrange("(t p) -> t p", p=P)
-            )
-        for name in ("c0", "c2", "c1"):
-            for g in range(PASSES):
-                load_weight(name, g)
-        ref_sb = []
-        for b in range(HALVES):
-            tile = keep.tile([P, M_TILES, HALF], F32, name=f"ref_{b}")
-            nc.sync.dma_start(
-                tile[:], ref[:, b * HALF : (b + 1) * HALF].rearrange("(h p) j -> p h j", p=P)
-            )
-            ref_sb.append(tile)
+        ref_sb = keep.tile([P, M_TILES, S], F32, name="ref_sb")
+        nc.sync.dma_start(ref_sb[:], ref.rearrange("(h p) j -> p h j", p=P))
 
         w_codes, w_scales = {}, {}
         grouped = {}
 
-        def cast(name, g):
-            tile = keep.tile([P, N, PACK], BF16, name=f"bf_{name}_{g}", align_bytes=64)
-            dst = tile[:].rearrange("p (c i) t -> p c t i", i=RUN)
+        def cast(name, g, tile):
+            dst = tile.rearrange("p (c i) t -> p c t i", i=RUN)
             src = raw[name, g][:].rearrange("p t (c i) -> p c t i", i=RUN)
             if (name, g) in ON_SCALAR:
                 nc.scalar.copy(dst, src)
             else:
                 nc.vector.tensor_copy(dst, src)
-            grouped[name, g] = tile
 
-        def quantize(name, g):
-            codes = keep.tile([P, N], U32, name=f"wq_{name}_{g}", align_bytes=64)
-            scales = keep.tile([P, N], U8, name=f"ws_{name}_{g}", align_bytes=64)
+        def quantize(name, passes, tile):
+            codes = keep.tile([P, len(passes), N], U32, name=f"wq_{name}_{passes[0]}", align_bytes=64)
+            scales = keep.tile([P, len(passes), N], U8, name=f"ws_{name}_{passes[0]}", align_bytes=64)
             nc.vector.quantize_mx(
-                out=codes[:].bitcast(FP8X4),
-                scales=scales[:],
-                in_=grouped[name, g][:].rearrange("p m t -> p (m t)"),
+                out=codes[:].rearrange("p g m -> p (g m)").bitcast(FP8X4),
+                scales=scales[:].rearrange("p g m -> p (g m)"),
+                in_=tile.rearrange("p g m t -> p (g m t)"),
             )
-            w_codes[name, g], w_scales[name, g] = codes, scales
+            for at, g in enumerate(passes):
+                w_codes[name, g], w_scales[name, g] = codes[:, at, :], scales[:, at, :]
+
+        def rounded(name, count, tag):
+            return keep.tile([P, count, N, PACK], BF16, name=name, tag=tag, align_bytes=64)
 
         x_codes = {}
+        picked = {}
 
         def gather_words(g, b):
-            tile = keep.tile([P, HALF], U32, name=f"xq_{g}_{b}", align_bytes=64)
+            if g not in picked:
+                picked[g] = keep.tile([P, S], U32, name=f"xq_{g}", tag=f"bf_d0_{g}", align_bytes=64)
+            tile = picked[g][:, b * HALF : (b + 1) * HALF]
             cols = offsets[:, b * (HALF // 16) : (b + 1) * (HALF // 16)]
-            nc.vector.tensor_copy(tile[:], word_table[g][:].bitcast(U32).indirect(cols))
+            nc.vector.tensor_copy(tile, word_table[g][:].bitcast(U32).indirect(cols))
             x_codes[g, b] = tile
 
         x_scale = keep.tile([P, S], U8, name="x_scale", align_bytes=64)
 
         def product(name, b):
-            bank = prod.tile([P, TILES, N], F32, name="bank")
-            for u in range(TILES):
-                j0 = b * HALF + u * P
-                for g in range(PASSES):
+            bank = prod.tile([P, TILES, N], F32, name=f"bank_{ORDER.index(name) % 2}_{b}")
+            for g in range(PASSES):
+                for u in range(TILES):
+                    j0 = b * HALF + u * P
                     nc.tensor.matmul_mx(
                         out=bank[:, u, :],
                         lhsT=x_codes[g, b][:, u * P : (u + 1) * P].bitcast(FP8X4),
                         lhsT_scale=x_scale[4 * g :, j0 : j0 + P],
-                        rhs=w_codes[name, g][:].bitcast(FP8X4),
-                        rhs_scale=w_scales[name, g][:],
-                        start=(g == 0),
-                        stop=(g == PASSES - 1),
+                        rhs=w_codes[name, g].bitcast(FP8X4),
+                        rhs_scale=w_scales[name, g],
+                        start=(g == 0 and u == 0),
+                        stop=(g == PASSES - 1 and u == TILES - 1),
                     )
             return bank
 
@@ -170,38 +166,34 @@ def tile_picked_yweno_err_p_kernel(
         def blocks(tile):
             return lambda u, h: tile[:, u, h * P : (h + 1) * P]
 
-        cast("d0", 0)
-        quantize("d0", 0)
+        first = [rounded(f"bf_d0_{g}", 1, f"bf_d0_{g}") for g in range(PASSES)]
+        cast("d0", 0, first[0][:, 0])
+        quantize("d0", [0], first[0][:])
         for b in range(HALVES):
             gather_words(0, b)
+        cast("d0", 1, first[1][:, 0])
         nc.vector.tensor_copy(x_scale[:], scale_table[:].indirect(offsets[:]))
-        cast("d0", 1)
-        quantize("d0", 1)
+        quantize("d0", [1], first[1][:])
         for b in range(HALVES):
             gather_words(1, b)
 
-        ideal_bank = sums.tile([P, TILES, N], F32, name="num_1")
-        nc.tensor.transpose(ideal_bank[:, 0, 0:P], ideal_rows[:], ident[:])
         ideal_cols = keep.tile([P, 12], F32, name="ideal_cols")
-        nc.scalar.copy(ideal_cols[:], ideal_bank[:, 0, 0:12])
 
         def ideal_col(i, b, u):
             c = 4 * i + b * TILES + u
             return ideal_cols[:, c : c + 1]
 
-        def inverse_smoothness(name, b):
+        def inverse_smoothness(name, b, sq, sq2):
             bank = product(name, b)
-            sq = work("sq_" + name, b)
-            nc.scalar.activation(sq[:], bank[:], ACT.Square)
-            sq2 = work("sq2_" + name, b)
-            nc.scalar.activation(sq2[:], sq[:], ACT.Square, bias=EPS)
+            nc.scalar.activation(sq, bank[:], ACT.Square)
+            nc.scalar.activation(sq2, sq, ACT.Square, bias=EPS)
             inv = work("inv_" + name, b)
-            nc.scalar.activation(inv[:], sq2[:], ACT.Abs_reciprocal_sqrt)
+            nc.scalar.activation(inv[:], sq2, ACT.Abs_reciprocal_sqrt)
             return inv
 
         def relative_weight(i, b, pivot_sq, inv):
-            ratio = work(f"ratio_{i}", b)
-            nc.vector.scalar_tensor_tensor(ratio[:], pivot_sq[:], EPS, inv[:], ALU.add, ALU.mult)
+            ratio = ratios[:, i // 2, b]
+            nc.vector.scalar_tensor_tensor(ratio, pivot_sq, EPS, inv[:], ALU.add, ALU.mult)
             weight = work(f"weight_{i}", b)
             for u in range(TILES):
                 nc.vector.scalar_tensor_tensor(
@@ -212,55 +204,69 @@ def tile_picked_yweno_err_p_kernel(
         den = [sums.tile([P, M_TILES, HALF], F32, name=f"den_{b}") for b in range(HALVES)]
         num = [sums.tile([P, M_TILES, HALF], F32, name=f"num_{b}") for b in range(HALVES)]
 
-        def prepare(name):
+        def prepare(name, tile):
             for g in range(PASSES):
-                cast(name, g)
-            for g in range(PASSES):
-                quantize(name, g)
+                cast(name, g, tile[:, g])
+            quantize(name, [0, 1], tile)
 
-        def weighted_term(name, b, weight, first):
-            bank = product(name, b)
+        def weighted_term(name, b, bank, weight):
             term = work("term_" + name, b)
             nc.vector.tensor_tensor(term[:], bank[:], weight[:], ALU.mult)
-            add_transposed(num[b], blocks(term), first, False)
+            return term
 
-        prepare("d1")
-        prepare("d2")
-        pivot_sq, weight0, weight2 = [], [], []
+        for name in ORDER[1:4]:
+            prepare(name, rounded("bf_" + name, PASSES, "bf_" + name)[:])
+        sq2_first = keep.tile([P, HALVES, TILES, N], F32, name="sq2_first", tag="squares")
+        inv0 = [inverse_smoothness("d0", b, work("sq_d0", b)[:], sq2_first[:, b]) for b in range(HALVES)]
+        ideal_bank = prod.tile([P, TILES, N], F32, name="bank_0_0")
+        nc.tensor.transpose(ideal_bank[:, 0, 0:P], ideal_rows[:], ident[:])
+        nc.scalar.copy(ideal_cols[:], ideal_bank[:, 0, 0:12])
+        squares = keep.tile([P, 2, HALVES, TILES, N], F32, name="squares", tag="squares")
         for b in range(HALVES):
-            inv0 = inverse_smoothness("d0", b)
-            bank = product("d1", b)
-            sq = work("sq_d1", b)
-            nc.scalar.activation(sq[:], bank[:], ACT.Square)
-            pivot_sq.append(sq)
-            weight0.append(relative_weight(0, b, sq, inv0))
-            add_transposed(den[b], lambda u, h: ideal_col(1, b, u).to_broadcast([P, P]), True, False)
-            add_transposed(den[b], blocks(weight0[b]), False, False)
+            nc.scalar.activation(squares[:, 0, b], product("d1", b)[:], ACT.Square)
+        rec0 = [product("c0", b) for b in range(HALVES)]
+        weight0, weight2 = [], []
+        ratios = keep.tile([P, 2, HALVES, TILES, N], F32, name="ratios", tag="bf_c0", align_bytes=64)
         for b in range(HALVES):
-            inv2 = inverse_smoothness("d2", b)
-            weight2.append(relative_weight(2, b, pivot_sq[b], inv2))
+            weight0.append(relative_weight(0, b, squares[:, 0, b], inv0[b]))
+            add_transposed(den[b], blocks(weight0[b]), True, False)
+            add_transposed(den[b], lambda u, h: ideal_col(1, b, u).to_broadcast([P, P]), False, False)
+        sq2_last = keep.tile([P, HALVES, TILES, N], F32, name="sq2_last", tag="late", align_bytes=64)
+        for b in range(HALVES):
+            inv2 = inverse_smoothness("d2", b, squares[:, 1, b], sq2_last[:, b])
+            weight2.append(relative_weight(2, b, squares[:, 0, b], inv2))
             add_transposed(den[b], blocks(weight2[b]), False, True)
-        prepare("c0")
-        prepare("c2")
-        prepare("c1")
+        late = rounded("late", 2 * PASSES, "late")
+        prepare("c1", late[:, 0:PASSES])
+        rec1 = [product("c1", b) for b in range(HALVES)]
+        term0 = [weighted_term("c0", b, rec0[b], weight0[b]) for b in range(HALVES)]
+        prepare("c2", late[:, PASSES:])
+        rec2 = [product("c2", b) for b in range(HALVES)]
         for b in range(HALVES):
-            root = work("root", b)
-            nc.scalar.activation(root[:], den[b][:], ACT.Abs_reciprocal_sqrt)
-            inv_den = work("inv_den", b)
-            nc.scalar.activation(inv_den[:], root[:], ACT.Square)
-            weighted_term("c0", b, weight0[b], True)
-            weighted_term("c2", b, weight2[b], False)
-            bank = product("c1", b)
+            add_transposed(num[b], blocks(term0[b]), True, False)
+        for b in range(HALVES):
+            bank = rec1[b]
             term = work("term_1", b)
             for u in range(TILES):
                 nc.scalar.activation(term[:, u, :], bank[:, u, :], ACT.Copy, scale=ideal_col(1, b, u))
-            add_transposed(num[b], blocks(term), False, True)
-            ref_den = work("ref_den", b)
-            nc.vector.tensor_tensor(ref_den[:], den[b][:], ref_sb[b][:], ALU.mult)
-            diff = work("diff", b)
-            nc.vector.tensor_tensor(diff[:], num[b][:], ref_den[:], ALU.subtract)
+            add_transposed(num[b], blocks(term), False, False)
+        ref_den, inv_den, diff, err = [], [], [], []
+        for b in range(HALVES):
+            ref_den.append(work("ref_den", b))
+            nc.vector.tensor_tensor(ref_den[b][:], den[b][:], ref_sb[:, :, b * HALF : (b + 1) * HALF], ALU.mult)
+        for b in range(HALVES):
+            add_transposed(num[b], blocks(weighted_term("c2", b, rec2[b], weight2[b])), False, True)
+        for b in range(HALVES):
+            root = work("root", b)
+            nc.scalar.activation(root[:], den[b][:], ACT.Abs_reciprocal_sqrt)
+            inv_den.append(work("inv_den", b))
+            nc.scalar.activation(inv_den[b][:], root[:], ACT.Square)
+        for b in range(HALVES):
+            diff.append(work("diff", b))
+            nc.vector.tensor_tensor(diff[b][:], num[b][:], ref_den[b][:], ALU.subtract)
+        for b in range(HALVES):
             err = work("err", b)
-            nc.vector.tensor_tensor(err[:], diff[:], inv_den[:], ALU.mult)
+            nc.vector.tensor_tensor(err[:], diff[b][:], inv_den[b][:], ALU.mult)
             res = work("res", b)
             nc.scalar.activation(res[:], err[:], ACT.Abs)
             nc.sync.dma_start(

@@ -26,9 +26,10 @@ TILES = HALF // P
 M_TILES = N // P
 EPS = 0.3
 RUN = 4
-ORDER = ("d0", "d1", "d2", "c0", "c1", "c2")
+PIN = "c0"
+ORDER = ("d0", "d1", "d2", "c0", "c2", "c1")
 
-ON_SCALAR = {("d0", 0), ("d0", 1), ("c2", 0), ("c2", 1), ("c1", 0), ("c1", 1)}
+ON_SCALAR = {("d0", 0), ("d0", 1)}
 
 
 def tile_picked_yweno_err_p_kernel(
@@ -183,92 +184,90 @@ def tile_picked_yweno_err_p_kernel(
             c = 4 * i + b * TILES + u
             return ideal_cols[:, c : c + 1]
 
-        def inverse_smoothness(name, b, sq, sq2):
-            bank = product(name, b)
-            nc.scalar.activation(sq, bank[:], ACT.Square)
+        def prepare(name):
+            tile = rounded("bf_" + name, PASSES, "bf_" + name)
+            for g in range(PASSES):
+                cast(name, g, tile[:, g])
+            quantize(name, [0, 1], tile[:])
+
+        def smoothness(name, b, sq, sq2):
+            nc.scalar.activation(sq, product(name, b)[:], ACT.Square)
             nc.scalar.activation(sq2, sq, ACT.Square, bias=EPS)
+
+        def invert(name, b, source):
+            root = work("root_" + name, b)
+            nc.scalar.activation(root[:], source, ACT.Abs_reciprocal_sqrt)
             inv = work("inv_" + name, b)
-            nc.scalar.activation(inv[:], sq2, ACT.Abs_reciprocal_sqrt)
+            nc.scalar.activation(inv[:], root[:], ACT.Square)
             return inv
 
-        def relative_weight(i, b, pivot_sq, inv):
-            ratio = ratios[:, i // 2, b]
-            nc.vector.scalar_tensor_tensor(ratio, pivot_sq, EPS, inv[:], ALU.add, ALU.mult)
-            weight = work(f"weight_{i}", b)
+        def relative_weight(i, b, weight, pivot, inv):
             for u in range(TILES):
                 nc.vector.scalar_tensor_tensor(
-                    weight[:, u, :], ratio[:, u, :], ideal_col(i, b, u), ratio[:, u, :], ALU.mult, ALU.mult
+                    weight[:, u, :], pivot[:, u, :], ideal_col(i, b, u), inv[:, u, :], ALU.mult, ALU.mult
                 )
-            return weight
+
+        def weighted_term(name, b, bank, weight):
+            term = work("term_" + name, b)
+            nc.vector.tensor_tensor(term[:], bank[:], weight, ALU.mult)
+            return term
 
         den = [sums.tile([P, M_TILES, HALF], F32, name=f"den_{b}") for b in range(HALVES)]
         num = [sums.tile([P, M_TILES, HALF], F32, name=f"num_{b}") for b in range(HALVES)]
 
-        def prepare(name, tile):
-            for g in range(PASSES):
-                cast(name, g, tile[:, g])
-            quantize(name, [0, 1], tile)
-
-        def weighted_term(name, b, bank, weight):
-            term = work("term_" + name, b)
-            nc.vector.tensor_tensor(term[:], bank[:], weight[:], ALU.mult)
-            return term
-
-        for name in ORDER[1:4]:
-            prepare(name, rounded("bf_" + name, PASSES, "bf_" + name)[:])
+        for name in ORDER[1:]:
+            prepare(name)
         sq2_first = keep.tile([P, HALVES, TILES, N], F32, name="sq2_first", tag="squares")
-        inv0 = [inverse_smoothness("d0", b, work("sq_d0", b)[:], sq2_first[:, b]) for b in range(HALVES)]
+        inv0 = []
+        for b in range(HALVES):
+            smoothness("d0", b, work("sq_d0", b)[:], sq2_first[:, b])
+            inv0.append(invert("d0", b, sq2_first[:, b]))
         ideal_bank = prod.tile([P, TILES, N], F32, name="bank_0_0")
         nc.tensor.transpose(ideal_bank[:, 0, 0:P], ideal_rows[:], ident[:])
         nc.scalar.copy(ideal_cols[:], ideal_bank[:, 0, 0:12])
         squares = keep.tile([P, 2, HALVES, TILES, N], F32, name="squares", tag="squares")
+        pivot = [work("pivot", b) for b in range(HALVES)]
         for b in range(HALVES):
-            nc.scalar.activation(squares[:, 0, b], product("d1", b)[:], ACT.Square)
+            smoothness("d1", b, squares[:, 0, b], pivot[b][:])
+        inv2 = []
+        for b in range(HALVES):
+            sq2 = work("sq2_d2", b)
+            smoothness("d2", b, squares[:, 1, b], sq2[:])
+            inv2.append(invert("d2", b, sq2[:]))
         rec0 = [product("c0", b) for b in range(HALVES)]
-        weight0, weight2 = [], []
-        ratios = keep.tile([P, 2, HALVES, TILES, N], F32, name="ratios", tag="bf_c0", align_bytes=64)
-        for b in range(HALVES):
-            weight0.append(relative_weight(0, b, squares[:, 0, b], inv0[b]))
-            add_transposed(den[b], blocks(weight0[b]), True, False)
-            add_transposed(den[b], lambda u, h: ideal_col(1, b, u).to_broadcast([P, P]), False, False)
-        sq2_last = keep.tile([P, HALVES, TILES, N], F32, name="sq2_last", tag="late", align_bytes=64)
-        for b in range(HALVES):
-            inv2 = inverse_smoothness("d2", b, squares[:, 1, b], sq2_last[:, b])
-            weight2.append(relative_weight(2, b, squares[:, 0, b], inv2))
-            add_transposed(den[b], blocks(weight2[b]), False, True)
-        late = rounded("late", 2 * PASSES, "late")
-        prepare("c1", late[:, 0:PASSES])
-        rec1 = [product("c1", b) for b in range(HALVES)]
-        term0 = [weighted_term("c0", b, rec0[b], weight0[b]) for b in range(HALVES)]
-        prepare("c2", late[:, PASSES:])
         rec2 = [product("c2", b) for b in range(HALVES)]
+        weights_rel = keep.tile([P, 2, HALVES, TILES, N], F32, name="weights_rel", tag="bf_" + PIN, align_bytes=64)
+        for b in range(HALVES):
+            relative_weight(0, b, weights_rel[:, 0, b], pivot[b], inv0[b])
+        term0 = [weighted_term("c0", b, rec0[b], weights_rel[:, 0, b]) for b in range(HALVES)]
+        rec1 = [product("c1", b) for b in range(HALVES)]
+        for b in range(HALVES):
+            add_transposed(den[b], blocks(weights_rel[:, 0, b]), True, False)
+            add_transposed(den[b], lambda u, h: ideal_col(1, b, u).to_broadcast([P, P]), False, False)
+        for b in range(HALVES):
+            relative_weight(2, b, weights_rel[:, 1, b], pivot[b], inv2[b])
+            add_transposed(den[b], blocks(weights_rel[:, 1, b]), False, True)
         for b in range(HALVES):
             add_transposed(num[b], blocks(term0[b]), True, False)
         for b in range(HALVES):
-            bank = rec1[b]
             term = work("term_1", b)
             for u in range(TILES):
-                nc.scalar.activation(term[:, u, :], bank[:, u, :], ACT.Copy, scale=ideal_col(1, b, u))
+                nc.scalar.activation(term[:, u, :], rec1[b][:, u, :], ACT.Copy, scale=ideal_col(1, b, u))
             add_transposed(num[b], blocks(term), False, False)
-        ref_den, inv_den, diff, err = [], [], [], []
+        for b in range(HALVES):
+            add_transposed(num[b], blocks(weighted_term("c2", b, rec2[b], weights_rel[:, 1, b])), False, True)
+        ref_den, diff = [], []
         for b in range(HALVES):
             ref_den.append(work("ref_den", b))
             nc.vector.tensor_tensor(ref_den[b][:], den[b][:], ref_sb[:, :, b * HALF : (b + 1) * HALF], ALU.mult)
-        for b in range(HALVES):
-            add_transposed(num[b], blocks(weighted_term("c2", b, rec2[b], weight2[b])), False, True)
-        for b in range(HALVES):
-            root = work("root", b)
-            nc.scalar.activation(root[:], den[b][:], ACT.Abs_reciprocal_sqrt)
-            inv_den.append(work("inv_den", b))
-            nc.scalar.activation(inv_den[b][:], root[:], ACT.Square)
+        inv_den = [invert("den", b, den[b][:]) for b in range(HALVES)]
         for b in range(HALVES):
             diff.append(work("diff", b))
             nc.vector.tensor_tensor(diff[b][:], num[b][:], ref_den[b][:], ALU.subtract)
         for b in range(HALVES):
             err = work("err", b)
-            nc.vector.tensor_tensor(err[:], diff[b][:], inv_den[b][:], ALU.mult)
             res = work("res", b)
-            nc.scalar.activation(res[:], err[:], ACT.Abs)
-            nc.sync.dma_start(
-                out[:, b * HALF : (b + 1) * HALF].rearrange("(h p) j -> p h j", p=P), res[:]
-            )
+            for h in range(M_TILES):
+                nc.vector.tensor_tensor(err[:, h, :], diff[b][:, h, :], inv_den[b][:, h, :], ALU.mult)
+                nc.scalar.activation(res[:, h, :], err[:, h, :], ACT.Abs)
+                nc.sync.dma_start(out[h * P : (h + 1) * P, b * HALF : (b + 1) * HALF], res[:, h, :])

@@ -20,31 +20,33 @@ P = 128
 PACK = 4
 K_PASS = P * PACK
 PASSES = K // K_PASS
+QUADRANTS = 4
+SCALE_ROWS = 4
+LIST_ROWS = 16
 HALVES = 2
 HALF = S // HALVES
 TILES = HALF // P
 M_TILES = N // P
+CANDIDATES = 3
 EPS = 0.3
 RUN = 4
-PIN = "c0"
-ORDER = ("d0", "d1", "d2", "c0", "c2", "c1")
 
-ON_SCALAR = {("d0", 0), ("d0", 1)}
+ORDER = ("d0", "d1", "d2", "c0", "c1", "c2")
 
 
 def tile_picked_yweno_err_p_kernel(
     tc, x_words, x_scales, wc0, wd0, ideal0, wc1, wd1, ideal1, wc2, wd2, ideal2, ref, offs, out
 ):
     nc = tc.nc
-    weights = {"d0": wd0, "d1": wd1, "d2": wd2, "c0": wc0, "c1": wc1, "c2": wc2}
+    matrices = {"d0": wd0, "d1": wd1, "d2": wd2, "c0": wc0, "c1": wc1, "c2": wc2}
     ideals = (ideal0, ideal1, ideal2)
 
     with ExitStack() as ctx:
         keep = ctx.enter_context(tc.tile_pool(name="keep", bufs=1))
-        prod = ctx.enter_context(tc.psum_pool(name="prod", bufs=1))
+        products = ctx.enter_context(tc.psum_pool(name="products", bufs=1))
         sums = ctx.enter_context(tc.psum_pool(name="sums", bufs=1))
 
-        offsets = keep.tile([P, S // 16], U16, name="offsets")
+        offsets = keep.tile([P, S // LIST_ROWS], U16, name="offsets")
         nc.sync.dma_start(offsets[:], offs)
 
         warm = keep.tile([P, 2], F32, name="warm")
@@ -59,89 +61,91 @@ def tile_picked_yweno_err_p_kernel(
 
         raw = {}
 
-        def load_weight(name, g, t0=0, t1=PACK):
-            if (name, g) not in raw:
-                raw[name, g] = keep.tile([P, PACK, N], F32, name=f"raw_{name}_{g}")
-            rows = weights[name][g * K_PASS : (g + 1) * K_PASS, :].rearrange("(p t) m -> p t m", t=PACK)
-            nc.sync.dma_start(raw[name, g][:, t0:t1, :], rows[:, t0:t1, :])
+        def load_weight(name, g):
+            raw[name, g] = keep.tile([P, PACK, N], F32, name=f"raw_{name}_{g}")
+            rows = matrices[name][g * K_PASS : (g + 1) * K_PASS, :]
+            nc.sync.dma_start(raw[name, g][:], rows.rearrange("(p t) m -> p t m", t=PACK))
 
         word_table = {}
 
-        def load_words(g, pieces=1):
-            tile = keep.tile([P, T], I32, name=f"word_table_{g}", align_bytes=64)
+        def load_words(g):
+            word_table[g] = keep.tile([P, T], I32, name=f"word_table_{g}", align_bytes=64)
             words = x_words[g].rearrange("p c t -> p (c t)").bitcast(I32)
-            step = T // pieces
-            for c0 in range(0, T, step):
-                nc.sync.dma_start(tile[:, c0 : c0 + step], words[:, c0 : c0 + step])
-            word_table[g] = tile
+            for c0 in range(0, T, T // 2):
+                nc.sync.dma_start(word_table[g][:, c0 : c0 + T // 2], words[:, c0 : c0 + T // 2])
 
-        for i in range(3):
+        stencil_tiles = HALVES * TILES
+        for i in range(CANDIDATES):
             nc.gpsimd.dma_start(
-                ideal_rows[4 * i : 4 * i + 4, :], ideals[i][0, :].rearrange("(t p) -> t p", p=P)
+                ideal_rows[stencil_tiles * i : stencil_tiles * (i + 1), :],
+                ideals[i][0, :].rearrange("(n p) -> n p", p=P),
             )
         make_identity(nc, ident[:])
+
         load_weight("d0", 0)
-        load_words(0, 2)
-        for q in range(4):
+        load_words(0)
+        for q in range(QUADRANTS):
             nc.sync.dma_start(
-                scale_table[32 * q : 32 * q + 4 * PASSES, :].bitcast(I32),
-                x_scales[:, 4 * q : 4 * q + 4, :].bitcast(I32),
+                scale_table[32 * q : 32 * q + SCALE_ROWS * PASSES, :].bitcast(I32),
+                x_scales[:, SCALE_ROWS * q : SCALE_ROWS * (q + 1), :].bitcast(I32),
             )
         load_weight("d0", 1)
-        load_words(1, 2)
+        load_words(1)
         for name in ORDER[1:]:
             for g in range(PASSES):
                 load_weight(name, g)
         ref_sb = keep.tile([P, M_TILES, S], F32, name="ref_sb")
         nc.sync.dma_start(ref_sb[:], ref.rearrange("(h p) j -> p h j", p=P))
 
+        def rounded(name, passes, tag):
+            return keep.tile([P, passes, N, PACK], BF16, name=name, tag=tag, align_bytes=64)
+
+        def interleave(copy, name, g, dst):
+            copy(
+                dst.rearrange("p (c i) t -> p c t i", i=RUN),
+                raw[name, g][:].rearrange("p t (c i) -> p c t i", i=RUN),
+            )
+
         w_codes, w_scales = {}, {}
-        grouped = {}
 
-        def cast(name, g, tile):
-            dst = tile.rearrange("p (c i) t -> p c t i", i=RUN)
-            src = raw[name, g][:].rearrange("p t (c i) -> p c t i", i=RUN)
-            if (name, g) in ON_SCALAR:
-                nc.scalar.copy(dst, src)
-            else:
-                nc.vector.tensor_copy(dst, src)
-
-        def quantize(name, passes, tile):
-            codes = keep.tile([P, len(passes), N], U32, name=f"wq_{name}_{passes[0]}", align_bytes=64)
-            scales = keep.tile([P, len(passes), N], U8, name=f"ws_{name}_{passes[0]}", align_bytes=64)
+        def quantize(name, passes, src):
+            codes = keep.tile([P, len(passes), N], U32, name=f"codes_{name}_{passes[0]}", align_bytes=64)
+            scales = keep.tile([P, len(passes), N], U8, name=f"scales_{name}_{passes[0]}", align_bytes=64)
             nc.vector.quantize_mx(
                 out=codes[:].rearrange("p g m -> p (g m)").bitcast(FP8X4),
                 scales=scales[:].rearrange("p g m -> p (g m)"),
-                in_=tile.rearrange("p g m t -> p (g m t)"),
+                in_=src.rearrange("p g m t -> p (g m t)"),
             )
             for at, g in enumerate(passes):
                 w_codes[name, g], w_scales[name, g] = codes[:, at, :], scales[:, at, :]
 
-        def rounded(name, count, tag):
-            return keep.tile([P, count, N, PACK], BF16, name=name, tag=tag, align_bytes=64)
+        def prepare_pass(copy, name, g, tag):
+            tile = rounded(f"bf_{name}_{g}", 1, tag)
+            interleave(copy, name, g, tile[:, 0])
+            quantize(name, [g], tile[:])
 
         x_codes = {}
-        picked = {}
 
-        def gather_words(g, b):
-            if g not in picked:
-                picked[g] = keep.tile([P, S], U32, name=f"xq_{g}", tag=f"bf_d0_{g}", align_bytes=64)
-            tile = picked[g][:, b * HALF : (b + 1) * HALF]
-            cols = offsets[:, b * (HALF // 16) : (b + 1) * (HALF // 16)]
-            nc.vector.tensor_copy(tile, word_table[g][:].bitcast(U32).indirect(cols))
-            x_codes[g, b] = tile
+        def gather_words(g):
+            x_codes[g] = keep.tile([P, S], U32, name=f"x_codes_{g}", tag=f"bf_d0_{g}", align_bytes=64)
+            per_half = HALF // LIST_ROWS
+            for b in range(HALVES):
+                entries = offsets[:, b * per_half : (b + 1) * per_half]
+                nc.vector.tensor_copy(
+                    x_codes[g][:, b * HALF : (b + 1) * HALF], word_table[g][:].bitcast(U32).indirect(entries)
+                )
 
         x_scale = keep.tile([P, S], U8, name="x_scale", align_bytes=64)
 
         def product(name, b):
-            bank = prod.tile([P, TILES, N], F32, name=f"bank_{ORDER.index(name) % 2}_{b}")
+            bank = products.tile([P, TILES, N], F32, name=f"bank_{ORDER.index(name) % 2}_{b}")
             for g in range(PASSES):
                 for u in range(TILES):
                     j0 = b * HALF + u * P
                     nc.tensor.matmul_mx(
                         out=bank[:, u, :],
-                        lhsT=x_codes[g, b][:, u * P : (u + 1) * P].bitcast(FP8X4),
-                        lhsT_scale=x_scale[4 * g :, j0 : j0 + P],
+                        lhsT=x_codes[g][:, j0 : j0 + P].bitcast(FP8X4),
+                        lhsT_scale=x_scale[SCALE_ROWS * g :, j0 : j0 + P],
                         rhs=w_codes[name, g].bitcast(FP8X4),
                         rhs_scale=w_scales[name, g],
                         start=(g == 0 and u == 0),
@@ -152,59 +156,42 @@ def tile_picked_yweno_err_p_kernel(
         def work(name, b):
             return keep.tile([P, TILES, N], F32, name=f"{name}_{b}")
 
-        def add_transposed(total, source, first, last):
+        def add_transposed(total, block, first, last):
             for u in range(TILES):
                 for h in range(M_TILES):
                     nc.tensor.matmul(
                         total[:, h, u * P : (u + 1) * P],
-                        source(u, h),
+                        block(u, h),
                         ident[:],
                         is_transpose=True,
                         start=(first and u == 0 and h == 0),
                         stop=(last and u == TILES - 1 and h == M_TILES - 1),
                     )
 
-        def blocks(tile):
-            return lambda u, h: tile[:, u, h * P : (h + 1) * P]
+        def blocks(values):
+            return lambda u, h: values[:, u, h * P : (h + 1) * P]
 
-        first = [rounded(f"bf_d0_{g}", 1, f"bf_d0_{g}") for g in range(PASSES)]
-        cast("d0", 0, first[0][:, 0])
-        quantize("d0", [0], first[0][:])
-        for b in range(HALVES):
-            gather_words(0, b)
-        cast("d0", 1, first[1][:, 0])
-        nc.vector.tensor_copy(x_scale[:], scale_table[:].indirect(offsets[:]))
-        quantize("d0", [1], first[1][:])
-        for b in range(HALVES):
-            gather_words(1, b)
-
-        ideal_cols = keep.tile([P, 12], F32, name="ideal_cols")
+        ideal_cols = keep.tile([P, CANDIDATES * stencil_tiles], F32, name="ideal_cols")
 
         def ideal_col(i, b, u):
-            c = 4 * i + b * TILES + u
+            c = stencil_tiles * i + b * TILES + u
             return ideal_cols[:, c : c + 1]
 
-        def prepare(name):
-            tile = rounded("bf_" + name, PASSES, "bf_" + name)
-            for g in range(PASSES):
-                cast(name, g, tile[:, g])
-            quantize(name, [0, 1], tile[:])
-
-        def smoothness(name, b, sq, sq2):
+        def smoothness(name, b, sq, y_sq):
             nc.scalar.activation(sq, product(name, b)[:], ACT.Square)
-            nc.scalar.activation(sq2, sq, ACT.Square, bias=EPS)
+            nc.scalar.activation(y_sq, sq, ACT.Square, bias=EPS)
 
-        def invert(name, b, source):
+        def invert(name, b, values):
             root = work("root_" + name, b)
-            nc.scalar.activation(root[:], source, ACT.Abs_reciprocal_sqrt)
-            inv = work("inv_" + name, b)
-            nc.scalar.activation(inv[:], root[:], ACT.Square)
-            return inv
+            nc.scalar.activation(root[:], values, ACT.Abs_reciprocal_sqrt)
+            inverse = work("inverse_" + name, b)
+            nc.scalar.activation(inverse[:], root[:], ACT.Square)
+            return inverse
 
-        def relative_weight(i, b, weight, pivot, inv):
+        def relative_weight(i, b, weight, y1_sq, inverse):
             for u in range(TILES):
                 nc.vector.scalar_tensor_tensor(
-                    weight[:, u, :], pivot[:, u, :], ideal_col(i, b, u), inv[:, u, :], ALU.mult, ALU.mult
+                    weight[:, u, :], y1_sq[:, u, :], ideal_col(i, b, u), inverse[:, u, :], ALU.mult, ALU.mult
                 )
 
         def weighted_term(name, b, bank, weight):
@@ -212,62 +199,84 @@ def tile_picked_yweno_err_p_kernel(
             nc.vector.tensor_tensor(term[:], bank[:], weight, ALU.mult)
             return term
 
+        prepare_pass(nc.scalar.copy, "d0", 0, "bf_d0_0")
+        gather_words(0)
+        d0_second = rounded("bf_d0_1", 1, "bf_d0_1")
+        interleave(nc.scalar.copy, "d0", 1, d0_second[:, 0])
+        nc.vector.tensor_copy(x_scale[:], scale_table[:].indirect(offsets[:]))
+        quantize("d0", [1], d0_second[:])
+        gather_words(1)
+
         den = [sums.tile([P, M_TILES, HALF], F32, name=f"den_{b}") for b in range(HALVES)]
         num = [sums.tile([P, M_TILES, HALF], F32, name=f"num_{b}") for b in range(HALVES)]
 
-        for name in ORDER[1:]:
-            prepare(name)
-        sq2_first = keep.tile([P, HALVES, TILES, N], F32, name="sq2_first", tag="squares")
-        inv0 = []
+        for name in ORDER[1:-1]:
+            tile = rounded("bf_" + name, PASSES, "bf_" + name)
+            for g in range(PASSES):
+                interleave(nc.vector.tensor_copy, name, g, tile[:, g])
+            quantize(name, list(range(PASSES)), tile[:])
+        prepare_pass(nc.vector.tensor_copy, "c2", 0, "bf_c2_0")
+
+        y0_sq = keep.tile([P, HALVES, TILES, N], F32, name="y0_sq", tag="squares")
+        inverse0 = []
         for b in range(HALVES):
-            smoothness("d0", b, work("sq_d0", b)[:], sq2_first[:, b])
-            inv0.append(invert("d0", b, sq2_first[:, b]))
-        ideal_bank = prod.tile([P, TILES, N], F32, name="bank_0_0")
+            smoothness("d0", b, work("sq_d0", b)[:], y0_sq[:, b])
+            inverse0.append(invert("d0", b, y0_sq[:, b]))
+
+        ideal_bank = products.tile([P, TILES, N], F32, name="bank_0_0")
         nc.tensor.transpose(ideal_bank[:, 0, 0:P], ideal_rows[:], ident[:])
-        nc.scalar.copy(ideal_cols[:], ideal_bank[:, 0, 0:12])
+        nc.scalar.copy(ideal_cols[:], ideal_bank[:, 0, 0 : CANDIDATES * stencil_tiles])
+
         squares = keep.tile([P, 2, HALVES, TILES, N], F32, name="squares", tag="squares")
-        pivot = [work("pivot", b) for b in range(HALVES)]
+        y1_sq = [work("y1_sq", b) for b in range(HALVES)]
         for b in range(HALVES):
-            smoothness("d1", b, squares[:, 0, b], pivot[b][:])
-        inv2 = []
+            smoothness("d1", b, squares[:, 0, b], y1_sq[b][:])
+        inverse2 = []
         for b in range(HALVES):
-            sq2 = work("sq2_d2", b)
-            smoothness("d2", b, squares[:, 1, b], sq2[:])
-            inv2.append(invert("d2", b, sq2[:]))
+            y2_sq = keep.tile([P, TILES, N], F32, name=f"y2_sq_{b}", align_bytes=64)
+            smoothness("d2", b, squares[:, 1, b], y2_sq[:])
+            inverse2.append(invert("d2", b, y2_sq[:]))
+
         rec0 = [product("c0", b) for b in range(HALVES)]
-        rec2 = [product("c2", b) for b in range(HALVES)]
-        weights_rel = keep.tile([P, 2, HALVES, TILES, N], F32, name="weights_rel", tag="bf_" + PIN, align_bytes=64)
-        for b in range(HALVES):
-            relative_weight(0, b, weights_rel[:, 0, b], pivot[b], inv0[b])
-        term0 = [weighted_term("c0", b, rec0[b], weights_rel[:, 0, b]) for b in range(HALVES)]
         rec1 = [product("c1", b) for b in range(HALVES)]
+
+        weight = keep.tile([P, 2, HALVES, TILES, N], F32, name="weight", tag="bf_c0", align_bytes=64)
         for b in range(HALVES):
-            add_transposed(den[b], blocks(weights_rel[:, 0, b]), True, False)
+            relative_weight(0, b, weight[:, 0, b], y1_sq[b], inverse0[b])
+        term0 = [weighted_term("c0", b, rec0[b], weight[:, 0, b]) for b in range(HALVES)]
+        for b in range(HALVES):
+            add_transposed(den[b], blocks(weight[:, 0, b]), True, False)
             add_transposed(den[b], lambda u, h: ideal_col(1, b, u).to_broadcast([P, P]), False, False)
         for b in range(HALVES):
-            relative_weight(2, b, weights_rel[:, 1, b], pivot[b], inv2[b])
-            add_transposed(den[b], blocks(weights_rel[:, 1, b]), False, True)
+            relative_weight(2, b, weight[:, 1, b], y1_sq[b], inverse2[b])
+            add_transposed(den[b], blocks(weight[:, 1, b]), False, True)
+
+        prepare_pass(nc.scalar.copy, "c2", 1, f"y2_sq_{HALVES - 1}")
+        rec2 = [product("c2", b) for b in range(HALVES)]
         for b in range(HALVES):
             add_transposed(num[b], blocks(term0[b]), True, False)
+        term1 = keep.tile([P, HALVES, TILES, N], F32, name="term1", tag="raw_c2_1")
         for b in range(HALVES):
-            term = work("term_1", b)
             for u in range(TILES):
-                nc.scalar.activation(term[:, u, :], rec1[b][:, u, :], ACT.Copy, scale=ideal_col(1, b, u))
-            add_transposed(num[b], blocks(term), False, False)
-        for b in range(HALVES):
-            add_transposed(num[b], blocks(weighted_term("c2", b, rec2[b], weights_rel[:, 1, b])), False, True)
+                nc.scalar.activation(term1[:, b, u, :], rec1[b][:, u, :], ACT.Copy, scale=ideal_col(1, b, u))
+            add_transposed(num[b], blocks(term1[:, b]), False, False)
+
         ref_den, diff = [], []
         for b in range(HALVES):
             ref_den.append(work("ref_den", b))
             nc.vector.tensor_tensor(ref_den[b][:], den[b][:], ref_sb[:, :, b * HALF : (b + 1) * HALF], ALU.mult)
-        inv_den = [invert("den", b, den[b][:]) for b in range(HALVES)]
+        for b in range(HALVES):
+            term2 = weighted_term("c2", b, rec2[b], weight[:, 1, b])
+            add_transposed(num[b], blocks(term2), False, True)
+        inverse_den = [invert("den", b, den[b][:]) for b in range(HALVES)]
         for b in range(HALVES):
             diff.append(work("diff", b))
             nc.vector.tensor_tensor(diff[b][:], num[b][:], ref_den[b][:], ALU.subtract)
+
         for b in range(HALVES):
             err = work("err", b)
-            res = work("res", b)
+            result = work("result", b)
             for h in range(M_TILES):
-                nc.vector.tensor_tensor(err[:, h, :], diff[b][:, h, :], inv_den[b][:, h, :], ALU.mult)
-                nc.scalar.activation(res[:, h, :], err[:, h, :], ACT.Abs)
-                nc.sync.dma_start(out[h * P : (h + 1) * P, b * HALF : (b + 1) * HALF], res[:, h, :])
+                nc.vector.tensor_tensor(err[:, h, :], diff[b][:, h, :], inverse_den[b][:, h, :], ALU.mult)
+                nc.scalar.activation(result[:, h, :], err[:, h, :], ACT.Abs)
+                nc.sync.dma_start(out[h * P : (h + 1) * P, b * HALF : (b + 1) * HALF], result[:, h, :])

from contextlib import ExitStack

import concourse.mybir as mybir
from concourse.masks import make_identity

K, T, S, N = 1024, 2048, 512, 256
FLOPS = 6 * 2 * K * N * S

F32 = mybir.dt.float32
BF16 = mybir.dt.bfloat16
I32 = mybir.dt.int32
U32 = mybir.dt.uint32
U16 = mybir.dt.uint16
U8 = mybir.dt.uint8
FP8X4 = mybir.dt.float8_e4m3fn_x4
ACT = mybir.ActivationFunctionType
ALU = mybir.AluOpType

P = 128
PACK = 4
K_PASS = P * PACK
PASSES = K // K_PASS
QUADRANTS = 4
SCALE_ROWS = 4
LIST_ROWS = 16
HALVES = 2
HALF = S // HALVES
TILES = HALF // P
M_TILES = N // P
CANDIDATES = 3
EPS = 0.3
RUN = 4

ORDER = ("d0", "d1", "d2", "c0", "c1", "c2")


def tile_picked_yweno_err_p_kernel(
    tc, x_words, x_scales, wc0, wd0, ideal0, wc1, wd1, ideal1, wc2, wd2, ideal2, ref, offs, out
):
    nc = tc.nc
    matrices = {"d0": wd0, "d1": wd1, "d2": wd2, "c0": wc0, "c1": wc1, "c2": wc2}
    ideals = (ideal0, ideal1, ideal2)

    with ExitStack() as ctx:
        keep = ctx.enter_context(tc.tile_pool(name="keep", bufs=1))
        products = ctx.enter_context(tc.psum_pool(name="products", bufs=1))
        sums = ctx.enter_context(tc.psum_pool(name="sums", bufs=1))

        offsets = keep.tile([P, S // LIST_ROWS], U16, name="offsets")
        nc.sync.dma_start(offsets[:], offs)

        warm = keep.tile([P, 2], F32, name="warm")
        nc.vector.memset(warm[:, 0:1], 1.0)
        nc.scalar.activation(warm[:, 1:2], warm[:, 0:1], ACT.Abs_reciprocal_sqrt)

        scale_table = keep.tile([P, T], U8, name="scale_table", align_bytes=64)
        nc.gpsimd.memset(scale_table[:].bitcast(I32), 0)
        ideal_rows = keep.tile([P, P], F32, name="ideal_rows")
        nc.gpsimd.memset(ideal_rows[:], 0.0)
        ident = keep.tile([P, P], F32, name="ident")

        raw = {}

        def load_weight(name, g):
            raw[name, g] = keep.tile([P, PACK, N], F32, name=f"raw_{name}_{g}")
            rows = matrices[name][g * K_PASS : (g + 1) * K_PASS, :]
            nc.sync.dma_start(raw[name, g][:], rows.rearrange("(p t) m -> p t m", t=PACK))

        word_table = {}

        def load_words(g):
            word_table[g] = keep.tile([P, T], I32, name=f"word_table_{g}", align_bytes=64)
            words = x_words[g].rearrange("p c t -> p (c t)").bitcast(I32)
            for c0 in range(0, T, T // 2):
                nc.sync.dma_start(word_table[g][:, c0 : c0 + T // 2], words[:, c0 : c0 + T // 2])

        stencil_tiles = HALVES * TILES
        for i in range(CANDIDATES):
            nc.gpsimd.dma_start(
                ideal_rows[stencil_tiles * i : stencil_tiles * (i + 1), :],
                ideals[i][0, :].rearrange("(n p) -> n p", p=P),
            )
        make_identity(nc, ident[:])

        load_weight("d0", 0)
        load_words(0)
        for q in range(QUADRANTS):
            nc.sync.dma_start(
                scale_table[32 * q : 32 * q + SCALE_ROWS * PASSES, :].bitcast(I32),
                x_scales[:, SCALE_ROWS * q : SCALE_ROWS * (q + 1), :].bitcast(I32),
            )
        load_weight("d0", 1)
        load_words(1)
        for name in ORDER[1:]:
            for g in range(PASSES):
                load_weight(name, g)
        ref_sb = keep.tile([P, M_TILES, S], F32, name="ref_sb")
        nc.sync.dma_start(ref_sb[:], ref.rearrange("(h p) j -> p h j", p=P))

        def rounded(name, passes, tag):
            return keep.tile([P, passes, N, PACK], BF16, name=name, tag=tag, align_bytes=64)

        def interleave(copy, name, g, dst):
            copy(
                dst.rearrange("p (c i) t -> p c t i", i=RUN),
                raw[name, g][:].rearrange("p t (c i) -> p c t i", i=RUN),
            )

        w_codes, w_scales = {}, {}

        def quantize(name, passes, src):
            codes = keep.tile([P, len(passes), N], U32, name=f"codes_{name}_{passes[0]}", align_bytes=64)
            scales = keep.tile([P, len(passes), N], U8, name=f"scales_{name}_{passes[0]}", align_bytes=64)
            nc.vector.quantize_mx(
                out=codes[:].rearrange("p g m -> p (g m)").bitcast(FP8X4),
                scales=scales[:].rearrange("p g m -> p (g m)"),
                in_=src.rearrange("p g m t -> p (g m t)"),
            )
            for at, g in enumerate(passes):
                w_codes[name, g], w_scales[name, g] = codes[:, at, :], scales[:, at, :]

        def prepare_pass(copy, name, g, tag):
            tile = rounded(f"bf_{name}_{g}", 1, tag)
            interleave(copy, name, g, tile[:, 0])
            quantize(name, [g], tile[:])

        x_codes = {}

        def gather_words(g):
            x_codes[g] = keep.tile([P, S], U32, name=f"x_codes_{g}", tag=f"bf_d0_{g}", align_bytes=64)
            per_half = HALF // LIST_ROWS
            for b in range(HALVES):
                entries = offsets[:, b * per_half : (b + 1) * per_half]
                nc.vector.tensor_copy(
                    x_codes[g][:, b * HALF : (b + 1) * HALF], word_table[g][:].bitcast(U32).indirect(entries)
                )

        x_scale = keep.tile([P, S], U8, name="x_scale", align_bytes=64)

        def product(name, b):
            bank = products.tile([P, TILES, N], F32, name=f"bank_{ORDER.index(name) % 2}_{b}")
            for g in range(PASSES):
                for u in range(TILES):
                    j0 = b * HALF + u * P
                    nc.tensor.matmul_mx(
                        out=bank[:, u, :],
                        lhsT=x_codes[g][:, j0 : j0 + P].bitcast(FP8X4),
                        lhsT_scale=x_scale[SCALE_ROWS * g :, j0 : j0 + P],
                        rhs=w_codes[name, g].bitcast(FP8X4),
                        rhs_scale=w_scales[name, g],
                        start=(g == 0 and u == 0),
                        stop=(g == PASSES - 1 and u == TILES - 1),
                    )
            return bank

        def work(name, b):
            return keep.tile([P, TILES, N], F32, name=f"{name}_{b}")

        def add_transposed(total, block, first, last):
            for u in range(TILES):
                for h in range(M_TILES):
                    nc.tensor.matmul(
                        total[:, h, u * P : (u + 1) * P],
                        block(u, h),
                        ident[:],
                        is_transpose=True,
                        start=(first and u == 0 and h == 0),
                        stop=(last and u == TILES - 1 and h == M_TILES - 1),
                    )

        def blocks(values):
            return lambda u, h: values[:, u, h * P : (h + 1) * P]

        ideal_cols = keep.tile([P, CANDIDATES * stencil_tiles], F32, name="ideal_cols")

        def ideal_col(i, b, u):
            c = stencil_tiles * i + b * TILES + u
            return ideal_cols[:, c : c + 1]

        def smoothness(name, b, sq, y_sq):
            nc.scalar.activation(sq, product(name, b)[:], ACT.Square)
            nc.scalar.activation(y_sq, sq, ACT.Square, bias=EPS)

        def invert(name, b, values):
            root = work("root_" + name, b)
            nc.scalar.activation(root[:], values, ACT.Abs_reciprocal_sqrt)
            inverse = work("inverse_" + name, b)
            nc.scalar.activation(inverse[:], root[:], ACT.Square)
            return inverse

        def relative_weight(i, b, weight, y1_sq, inverse):
            for u in range(TILES):
                nc.vector.scalar_tensor_tensor(
                    weight[:, u, :], y1_sq[:, u, :], ideal_col(i, b, u), inverse[:, u, :], ALU.mult, ALU.mult
                )

        def weighted_term(name, b, bank, weight):
            term = work("term_" + name, b)
            nc.vector.tensor_tensor(term[:], bank[:], weight, ALU.mult)
            return term

        prepare_pass(nc.scalar.copy, "d0", 0, "bf_d0_0")
        gather_words(0)
        d0_second = rounded("bf_d0_1", 1, "bf_d0_1")
        interleave(nc.scalar.copy, "d0", 1, d0_second[:, 0])
        nc.vector.tensor_copy(x_scale[:], scale_table[:].indirect(offsets[:]))
        quantize("d0", [1], d0_second[:])
        gather_words(1)

        den = [sums.tile([P, M_TILES, HALF], F32, name=f"den_{b}") for b in range(HALVES)]
        num = [sums.tile([P, M_TILES, HALF], F32, name=f"num_{b}") for b in range(HALVES)]

        for name in ORDER[1:-1]:
            tile = rounded("bf_" + name, PASSES, "bf_" + name)
            for g in range(PASSES):
                interleave(nc.vector.tensor_copy, name, g, tile[:, g])
            quantize(name, list(range(PASSES)), tile[:])
        prepare_pass(nc.vector.tensor_copy, "c2", 0, "bf_c2_0")

        y0_sq = keep.tile([P, HALVES, TILES, N], F32, name="y0_sq", tag="squares")
        inverse0 = []
        for b in range(HALVES):
            smoothness("d0", b, work("sq_d0", b)[:], y0_sq[:, b])
            inverse0.append(invert("d0", b, y0_sq[:, b]))

        ideal_bank = products.tile([P, TILES, N], F32, name="bank_0_0")
        nc.tensor.transpose(ideal_bank[:, 0, 0:P], ideal_rows[:], ident[:])
        nc.scalar.copy(ideal_cols[:], ideal_bank[:, 0, 0 : CANDIDATES * stencil_tiles])

        squares = keep.tile([P, 2, HALVES, TILES, N], F32, name="squares", tag="squares")
        y1_sq = [work("y1_sq", b) for b in range(HALVES)]
        for b in range(HALVES):
            smoothness("d1", b, squares[:, 0, b], y1_sq[b][:])
        inverse2 = []
        for b in range(HALVES):
            y2_sq = keep.tile([P, TILES, N], F32, name=f"y2_sq_{b}", align_bytes=64)
            smoothness("d2", b, squares[:, 1, b], y2_sq[:])
            inverse2.append(invert("d2", b, y2_sq[:]))

        rec0 = [product("c0", b) for b in range(HALVES)]
        rec1 = [product("c1", b) for b in range(HALVES)]

        weight = keep.tile([P, 2, HALVES, TILES, N], F32, name="weight", tag="bf_c0", align_bytes=64)
        for b in range(HALVES):
            relative_weight(0, b, weight[:, 0, b], y1_sq[b], inverse0[b])
        term0 = [weighted_term("c0", b, rec0[b], weight[:, 0, b]) for b in range(HALVES)]
        for b in range(HALVES):
            add_transposed(den[b], blocks(weight[:, 0, b]), True, False)
            add_transposed(den[b], lambda u, h: ideal_col(1, b, u).to_broadcast([P, P]), False, False)
        for b in range(HALVES):
            relative_weight(2, b, weight[:, 1, b], y1_sq[b], inverse2[b])
            add_transposed(den[b], blocks(weight[:, 1, b]), False, True)

        prepare_pass(nc.scalar.copy, "c2", 1, f"y2_sq_{HALVES - 1}")
        rec2 = [product("c2", b) for b in range(HALVES)]
        for b in range(HALVES):
            add_transposed(num[b], blocks(term0[b]), True, False)
        term1 = keep.tile([P, HALVES, TILES, N], F32, name="term1", tag="raw_c2_1")
        for b in range(HALVES):
            for u in range(TILES):
                nc.scalar.activation(term1[:, b, u, :], rec1[b][:, u, :], ACT.Copy, scale=ideal_col(1, b, u))
            add_transposed(num[b], blocks(term1[:, b]), False, False)

        ref_den, diff = [], []
        for b in range(HALVES):
            ref_den.append(work("ref_den", b))
            nc.vector.tensor_tensor(ref_den[b][:], den[b][:], ref_sb[:, :, b * HALF : (b + 1) * HALF], ALU.mult)
        for b in range(HALVES):
            term2 = weighted_term("c2", b, rec2[b], weight[:, 1, b])
            add_transposed(num[b], blocks(term2), False, True)
        inverse_den = [invert("den", b, den[b][:]) for b in range(HALVES)]
        for b in range(HALVES):
            diff.append(work("diff", b))
            nc.vector.tensor_tensor(diff[b][:], num[b][:], ref_den[b][:], ALU.subtract)

        for b in range(HALVES):
            err = work("err", b)
            result = work("result", b)
            for h in range(M_TILES):
                nc.vector.tensor_tensor(err[:, h, :], diff[b][:, h, :], inverse_den[b][:, h, :], ALU.mult)
                nc.scalar.activation(result[:, h, :], err[:, h, :], ACT.Abs)
                nc.sync.dma_start(out[h * P : (h + 1) * P, b * HALF : (b + 1) * HALF], result[:, h, :])
